import numpy as np, ml_dtypes
CORES = [3,19,35,51,67,83,99,115]
N = 8
def setup_inputs(rng):
    return {"x": rng.standard_normal((N, 128, 8192), dtype=np.float32).astype(ml_dtypes.bfloat16)}
def reference(x):
    s = x.sum(axis=0, dtype=np.float64).astype(x.dtype)
    return {"y": np.broadcast_to(s, (N,) + s.shape)}

@@ -1,0 +1,130 @@
+import concourse.bass as bass
+
+STAGES = [128]
+S = 8
+RAILS = False
+NR = 1
+PRE = 2
+
+K = len(STAGES)
+OFF = [sum(STAGES[:k]) for k in range(K)]
+SIZES = sorted(set(STAGES))
+CLS = [SIZES.index(r) for r in STAGES]
+IDX = [CLS[:k].count(CLS[k]) for k in range(K)]
+
+
+def shape_of(c):
+    if c >= len(SIZES):
+        return [1, 128, 1]
+    return [CLS.count(c) * S, 128, SIZES[c] * 8192 // (S * 128)]
+
+
+SCRATCH = {
+    "xa": ("dram", shape_of(0), "bfloat16"), "ra": ("dram", shape_of(0), "bfloat16"),
+    "xb": ("dram", shape_of(1), "bfloat16"), "rb": ("dram", shape_of(1), "bfloat16"),
+    "xc": ("dram", shape_of(2), "bfloat16"), "rc": ("dram", shape_of(2), "bfloat16"),
+}
+SEMAPHORES = ["st", "sent"] + ["s%d" % k for k in range(16)] + ["ld%d" % k for k in range(16)]
+
+
+def red_core(k, s):
+    if RAILS:
+        j, h = divmod(s, 2)
+        return (2 * j + 1) * 8 + (6 if h else 2) + k % 2
+    return 2 * s * 8 + 4 + (3 - k % NR)
+
+
+def fwd_core(rank_core, s):
+    if RAILS and s % 2:
+        return (rank_core // 8) * 8 + 6 + (s // 2) % 2
+    return None
+
+
+def bits(first, n):
+    return ((1 << n) - 1) << first
+
+
+def rank_program(g, core, T, topo):
+    sems = [T.sem.s0, T.sem.s1, T.sem.s2, T.sem.s3, T.sem.s4, T.sem.s5, T.sem.s6, T.sem.s7,
+            T.sem.s8, T.sem.s9, T.sem.s10, T.sem.s11, T.sem.s12, T.sem.s13, T.sem.s14, T.sem.s15]
+    lds = [T.sem.ld0, T.sem.ld1, T.sem.ld2, T.sem.ld3, T.sem.ld4, T.sem.ld5, T.sem.ld6, T.sem.ld7,
+           T.sem.ld8, T.sem.ld9, T.sem.ld10, T.sem.ld11, T.sem.ld12, T.sem.ld13, T.sem.ld14, T.sem.ld15]
+    xbuf = [T.xa, T.xb, T.xc]
+    rbuf = [T.ra, T.rb, T.rc]
+    ranks = list(T.cores)
+
+    def piece(k, s):
+        return xbuf[CLS[k]][IDX[k] * S + s]
+
+    def landed(k, i):
+        return xbuf[CLS[k]][IDX[k] * 8 + i]
+
+    def did(c):
+        rid, pid, se = topo.addr(c)
+        return bass.DstId(rid=rid, pnc=pid)
+
+    def copy(src, dst, dst_core, mask, sem):
+        return bass.RemoteDMATransfer(dst_ids=[did(dst_core)], dma_engine_mask=mask, remote_sem=sem,
+                                      src=src, dst=dst)
+
+    direct = [s for s in range(S) if fwd_core(ranks[0], s) is None]
+    passed = [s for s in range(S) if fwd_core(ranks[0], s) is not None]
+    e_dir = 8 // len(direct)
+    e_pas = 8 // len(passed) if passed else 0
+    sent = 0
+    rank = T.rank_of(core)
+
+    if rank is not None:
+        def load(k):
+            g.dma_start(xbuf[CLS[k]][IDX[k] * S:(IDX[k] + 1) * S],
+                        T.x[OFF[k]:OFF[k] + STAGES[k], :]).then_inc(lds[k], 16)
+
+        for k in range(min(PRE, K)):
+            load(k)
+        for k in range(K):
+            g.wait_ge(lds[k], 16)
+            tr = []
+            for n, s in enumerate(direct):
+                tr.append(copy(piece(k, s), landed(k, rank), red_core(k, s), bits(n * e_dir, e_dir), sems[k]))
+                sent += e_dir
+            for n, s in enumerate(passed):
+                tr.append(copy(piece(k, s), piece(k, s), fwd_core(core, s), bits(8 + n * e_pas, e_pas), sems[k]))
+                sent += e_pas
+            g.remote_dma_fused(tr, local_sem=T.sem.sent)
+            if k + PRE < K:
+                load(k + PRE)
+        for k in range(K):
+            g.wait_ge(sems[k], 8 * S)
+            g.dma_start(T.y[OFF[k]:OFF[k] + STAGES[k], :],
+                        rbuf[CLS[k]][IDX[k] * S:(IDX[k] + 1) * S]).then_inc(T.sem.st, 16)
+        g.wait_ge(T.sem.st, 16 * K)
+        g.wait_ge(T.sem.sent, sent)
+        return
+
+    home = [r for r in ranks if r // 8 == core // 8]
+    mine = [s for s in passed if home and fwd_core(home[0], s) == core]
+    if mine:
+        e_fwd = 8 // len(mine)
+        i = T.rank_of(home[0])
+        for k in range(K):
+            g.wait_ge(sems[k], e_pas * len(mine))
+            tr = [copy(piece(k, s), landed(k, i), red_core(k, s), bits(n * e_fwd, e_fwd), sems[k])
+                  for n, s in enumerate(mine)]
+            sent += e_fwd * len(mine)
+            g.remote_dma_fused(tr, local_sem=T.sem.sent)
+        g.wait_ge(T.sem.sent, sent)
+        return
+
+    n_fwd = len([s for s in passed if fwd_core(ranks[0], s) == fwd_core(ranks[0], passed[0])]) if passed else 1
+    for k in range(K):
+        for s in range(S):
+            if red_core(k, s) != core:
+                continue
+            g.wait_ge(sems[k], 8 * (e_dir if s in direct else 8 // n_fwd))
+            g.remote_dma_fused([bass.RemoteDMATransfer(
+                dst_ids=[did(r) for r in ranks], dma_engine_mask=0xFF, remote_sem=sems[k],
+                srcs=[landed(k, i) for i in range(8)],
+                dsts=[rbuf[CLS[k]][IDX[k] * S + s] for r in ranks], alu_op=1)], local_sem=T.sem.sent)
+            sent += 8
+    if sent:
+        g.wait_ge(T.sem.sent, sent)

@@ -1,6 +1,6 @@
 import concourse.bass as bass
 
-STAGES = [128]
+STAGES = [16] * 8
 S = 8
 RAILS = False
 NR = 1

@@ -1,8 +1,8 @@
 import concourse.bass as bass
 
-STAGES = [16] * 8
-S = 8
-RAILS = False
+STAGES = [32] * 4
+S = 16
+RAILS = True
 NR = 1
 PRE = 2
 

@@ -1,6 +1,6 @@
 import concourse.bass as bass
 
-STAGES = [32] * 4
+STAGES = [16] * 8
 S = 16
 RAILS = True
 NR = 1

@@ -1,43 +1,25 @@
 import concourse.bass as bass
 
-STAGES = [16] * 8
+K = 8
+ROWS = 128 // K
 S = 16
-RAILS = True
-NR = 1
+W = ROWS * 8192 // (S * 128)
 PRE = 2
 
-K = len(STAGES)
-OFF = [sum(STAGES[:k]) for k in range(K)]
-SIZES = sorted(set(STAGES))
-CLS = [SIZES.index(r) for r in STAGES]
-IDX = [CLS[:k].count(CLS[k]) for k in range(K)]
-
-
-def shape_of(c):
-    if c >= len(SIZES):
-        return [1, 128, 1]
-    return [CLS.count(c) * S, 128, SIZES[c] * 8192 // (S * 128)]
-
-
 SCRATCH = {
-    "xa": ("dram", shape_of(0), "bfloat16"), "ra": ("dram", shape_of(0), "bfloat16"),
-    "xb": ("dram", shape_of(1), "bfloat16"), "rb": ("dram", shape_of(1), "bfloat16"),
-    "xc": ("dram", shape_of(2), "bfloat16"), "rc": ("dram", shape_of(2), "bfloat16"),
+    "xa": ("dram", [K * S, 128, W], "bfloat16"),
+    "ra": ("dram", [K * S, 128, W], "bfloat16"),
 }
-SEMAPHORES = ["st", "sent"] + ["s%d" % k for k in range(16)] + ["ld%d" % k for k in range(16)]
+SEMAPHORES = ["st", "sent"] + ["s%d" % k for k in range(8)] + ["ld%d" % k for k in range(8)]
 
 
 def red_core(k, s):
-    if RAILS:
-        j, h = divmod(s, 2)
-        return (2 * j + 1) * 8 + (6 if h else 2) + k % 2
-    return 2 * s * 8 + 4 + (3 - k % NR)
+    j, h = divmod(s, 2)
+    return (2 * j + 1) * 8 + (6 if h else 2) + k % 2
 
 
-def fwd_core(rank_core, s):
-    if RAILS and s % 2:
-        return (rank_core // 8) * 8 + 6 + (s // 2) % 2
-    return None
+def fwd_off(s):
+    return 6 + (s // 2) % 2 if s % 2 else None
 
 
 def bits(first, n):
@@ -45,19 +27,15 @@ def bits(first, n):
 
 
 def rank_program(g, core, T, topo):
-    sems = [T.sem.s0, T.sem.s1, T.sem.s2, T.sem.s3, T.sem.s4, T.sem.s5, T.sem.s6, T.sem.s7,
-            T.sem.s8, T.sem.s9, T.sem.s10, T.sem.s11, T.sem.s12, T.sem.s13, T.sem.s14, T.sem.s15]
-    lds = [T.sem.ld0, T.sem.ld1, T.sem.ld2, T.sem.ld3, T.sem.ld4, T.sem.ld5, T.sem.ld6, T.sem.ld7,
-           T.sem.ld8, T.sem.ld9, T.sem.ld10, T.sem.ld11, T.sem.ld12, T.sem.ld13, T.sem.ld14, T.sem.ld15]
-    xbuf = [T.xa, T.xb, T.xc]
-    rbuf = [T.ra, T.rb, T.rc]
+    sems = [T.sem.s0, T.sem.s1, T.sem.s2, T.sem.s3, T.sem.s4, T.sem.s5, T.sem.s6, T.sem.s7]
+    lds = [T.sem.ld0, T.sem.ld1, T.sem.ld2, T.sem.ld3, T.sem.ld4, T.sem.ld5, T.sem.ld6, T.sem.ld7]
     ranks = list(T.cores)
 
     def piece(k, s):
-        return xbuf[CLS[k]][IDX[k] * S + s]
+        return T.xa[k * S + s]
 
     def landed(k, i):
-        return xbuf[CLS[k]][IDX[k] * 8 + i]
+        return T.xa[k * 8 + i]
 
     def did(c):
         rid, pid, se = topo.addr(c)
@@ -67,64 +45,62 @@ def rank_program(g, core, T, topo):
         return bass.RemoteDMATransfer(dst_ids=[did(dst_core)], dma_engine_mask=mask, remote_sem=sem,
                                       src=src, dst=dst)
 
-    direct = [s for s in range(S) if fwd_core(ranks[0], s) is None]
-    passed = [s for s in range(S) if fwd_core(ranks[0], s) is not None]
+    direct = [s for s in range(S) if fwd_off(s) is None]
+    passed = [s for s in range(S) if fwd_off(s) is not None]
     e_dir = 8 // len(direct)
-    e_pas = 8 // len(passed) if passed else 0
+    e_pas = 8 // len(passed)
+
+    def e_fwd(off):
+        return 8 // len([s for s in passed if fwd_off(s) == off])
+
     sent = 0
     rank = T.rank_of(core)
 
     if rank is not None:
         def load(k):
-            g.dma_start(xbuf[CLS[k]][IDX[k] * S:(IDX[k] + 1) * S],
-                        T.x[OFF[k]:OFF[k] + STAGES[k], :]).then_inc(lds[k], 16)
+            if k < K:
+                g.dma_start(T.xa[k * S:(k + 1) * S], T.x[k * ROWS:(k + 1) * ROWS, :]).then_inc(lds[k], 16)
 
-        for k in range(min(PRE, K)):
+        for k in range(PRE):
             load(k)
         for k in range(K):
             g.wait_ge(lds[k], 16)
-            tr = []
-            for n, s in enumerate(direct):
-                tr.append(copy(piece(k, s), landed(k, rank), red_core(k, s), bits(n * e_dir, e_dir), sems[k]))
-                sent += e_dir
-            for n, s in enumerate(passed):
-                tr.append(copy(piece(k, s), piece(k, s), fwd_core(core, s), bits(8 + n * e_pas, e_pas), sems[k]))
-                sent += e_pas
+            tr = [copy(piece(k, s), landed(k, rank), red_core(k, s), bits(n * e_dir, e_dir), sems[k])
+                  for n, s in enumerate(direct)]
+            tr += [copy(piece(k, s), piece(k, s), core - core % 8 + fwd_off(s), bits(8 + n * e_pas, e_pas), sems[k])
+                   for n, s in enumerate(passed)]
+            sent += e_dir * len(direct) + e_pas * len(passed)
             g.remote_dma_fused(tr, local_sem=T.sem.sent)
-            if k + PRE < K:
-                load(k + PRE)
+            load(k + PRE)
         for k in range(K):
             g.wait_ge(sems[k], 8 * S)
-            g.dma_start(T.y[OFF[k]:OFF[k] + STAGES[k], :],
-                        rbuf[CLS[k]][IDX[k] * S:(IDX[k] + 1) * S]).then_inc(T.sem.st, 16)
+            g.dma_start(T.y[k * ROWS:(k + 1) * ROWS, :], T.ra[k * S:(k + 1) * S]).then_inc(T.sem.st, 16)
         g.wait_ge(T.sem.st, 16 * K)
         g.wait_ge(T.sem.sent, sent)
         return
 
     home = [r for r in ranks if r // 8 == core // 8]
-    mine = [s for s in passed if home and fwd_core(home[0], s) == core]
+    mine = [s for s in passed if home and fwd_off(s) == core % 8]
     if mine:
-        e_fwd = 8 // len(mine)
+        e = e_fwd(core % 8)
         i = T.rank_of(home[0])
         for k in range(K):
             g.wait_ge(sems[k], e_pas * len(mine))
-            tr = [copy(piece(k, s), landed(k, i), red_core(k, s), bits(n * e_fwd, e_fwd), sems[k])
-                  for n, s in enumerate(mine)]
-            sent += e_fwd * len(mine)
-            g.remote_dma_fused(tr, local_sem=T.sem.sent)
+            g.remote_dma_fused([copy(piece(k, s), landed(k, i), red_core(k, s), bits(n * e, e), sems[k])
+                                for n, s in enumerate(mine)], local_sem=T.sem.sent)
+            sent += e * len(mine)
         g.wait_ge(T.sem.sent, sent)
         return
 
-    n_fwd = len([s for s in passed if fwd_core(ranks[0], s) == fwd_core(ranks[0], passed[0])]) if passed else 1
     for k in range(K):
         for s in range(S):
             if red_core(k, s) != core:
                 continue
-            g.wait_ge(sems[k], 8 * (e_dir if s in direct else 8 // n_fwd))
+            g.wait_ge(sems[k], 8 * (e_dir if s in direct else e_fwd(fwd_off(s))))
             g.remote_dma_fused([bass.RemoteDMATransfer(
                 dst_ids=[did(r) for r in ranks], dma_engine_mask=0xFF, remote_sem=sems[k],
                 srcs=[landed(k, i) for i in range(8)],
-                dsts=[rbuf[CLS[k]][IDX[k] * S + s] for r in ranks], alu_op=1)], local_sem=T.sem.sent)
+                dsts=[T.ra[k * S + s] for r in ranks], alu_op=1)], local_sem=T.sem.sent)
             sent += 8
     if sent:
         g.wait_ge(T.sem.sent, sent)

import concourse.bass as bass

K = 8
ROWS = 128 // K
S = 16
W = ROWS * 8192 // (S * 128)
PRE = 2

SCRATCH = {
    "xa": ("dram", [K * S, 128, W], "bfloat16"),
    "ra": ("dram", [K * S, 128, W], "bfloat16"),
}
SEMAPHORES = ["st", "sent"] + ["s%d" % k for k in range(8)] + ["ld%d" % k for k in range(8)]


def red_core(k, s):
    j, h = divmod(s, 2)
    return (2 * j + 1) * 8 + (6 if h else 2) + k % 2


def fwd_off(s):
    return 6 + (s // 2) % 2 if s % 2 else None


def bits(first, n):
    return ((1 << n) - 1) << first


def rank_program(g, core, T, topo):
    sems = [T.sem.s0, T.sem.s1, T.sem.s2, T.sem.s3, T.sem.s4, T.sem.s5, T.sem.s6, T.sem.s7]
    lds = [T.sem.ld0, T.sem.ld1, T.sem.ld2, T.sem.ld3, T.sem.ld4, T.sem.ld5, T.sem.ld6, T.sem.ld7]
    ranks = list(T.cores)

    def piece(k, s):
        return T.xa[k * S + s]

    def landed(k, i):
        return T.xa[k * 8 + i]

    def did(c):
        rid, pid, se = topo.addr(c)
        return bass.DstId(rid=rid, pnc=pid)

    def copy(src, dst, dst_core, mask, sem):
        return bass.RemoteDMATransfer(dst_ids=[did(dst_core)], dma_engine_mask=mask, remote_sem=sem,
                                      src=src, dst=dst)

    direct = [s for s in range(S) if fwd_off(s) is None]
    passed = [s for s in range(S) if fwd_off(s) is not None]
    e_dir = 8 // len(direct)
    e_pas = 8 // len(passed)

    def e_fwd(off):
        return 8 // len([s for s in passed if fwd_off(s) == off])

    sent = 0
    rank = T.rank_of(core)

    if rank is not None:
        def load(k):
            if k < K:
                g.dma_start(T.xa[k * S:(k + 1) * S], T.x[k * ROWS:(k + 1) * ROWS, :]).then_inc(lds[k], 16)

        for k in range(PRE):
            load(k)
        for k in range(K):
            g.wait_ge(lds[k], 16)
            tr = [copy(piece(k, s), landed(k, rank), red_core(k, s), bits(n * e_dir, e_dir), sems[k])
                  for n, s in enumerate(direct)]
            tr += [copy(piece(k, s), piece(k, s), core - core % 8 + fwd_off(s), bits(8 + n * e_pas, e_pas), sems[k])
                   for n, s in enumerate(passed)]
            sent += e_dir * len(direct) + e_pas * len(passed)
            g.remote_dma_fused(tr, local_sem=T.sem.sent)
            load(k + PRE)
        for k in range(K):
            g.wait_ge(sems[k], 8 * S)
            g.dma_start(T.y[k * ROWS:(k + 1) * ROWS, :], T.ra[k * S:(k + 1) * S]).then_inc(T.sem.st, 16)
        g.wait_ge(T.sem.st, 16 * K)
        g.wait_ge(T.sem.sent, sent)
        return

    home = [r for r in ranks if r // 8 == core // 8]
    mine = [s for s in passed if home and fwd_off(s) == core % 8]
    if mine:
        e = e_fwd(core % 8)
        i = T.rank_of(home[0])
        for k in range(K):
            g.wait_ge(sems[k], e_pas * len(mine))
            g.remote_dma_fused([copy(piece(k, s), landed(k, i), red_core(k, s), bits(n * e, e), sems[k])
                                for n, s in enumerate(mine)], local_sem=T.sem.sent)
            sent += e * len(mine)
        g.wait_ge(T.sem.sent, sent)
        return

    for k in range(K):
        for s in range(S):
            if red_core(k, s) != core:
                continue
            g.wait_ge(sems[k], 8 * (e_dir if s in direct else e_fwd(fwd_off(s))))
            g.remote_dma_fused([bass.RemoteDMATransfer(
                dst_ids=[did(r) for r in ranks], dma_engine_mask=0xFF, remote_sem=sems[k],
                srcs=[landed(k, i) for i in range(8)],
                dsts=[T.ra[k * S + s] for r in ranks], alu_op=1)], local_sem=T.sem.sent)
            sent += 8
    if sent:
        g.wait_ge(T.sem.sent, sent)
